import numpy as np
import ml_dtypes


def mxq(x, axis, fmt="e4m3"):
    dtype, down = {"e4m3": (ml_dtypes.float8_e4m3fn, 7), "e5m2": (ml_dtypes.float8_e5m2, 14)}[fmt]
    v = np.moveaxis(np.asarray(x, np.float32).astype(ml_dtypes.bfloat16).astype(np.float64), axis, -1)
    blocks = v.reshape(v.shape[:-1] + (-1, 32))
    amax = np.abs(blocks).max(-1, keepdims=True)
    byte = np.maximum(np.where(amax > 0, np.frexp(amax)[1] - 1 + 127, 0) - down, 1)
    scale = np.exp2(byte - 127.0)
    codes = (blocks / scale).astype(np.float32).astype(dtype).astype(np.float64)
    return np.moveaxis((codes * scale).reshape(v.shape), -1, axis)


WIDE = False


def mx_kscale(k, group=512):
    if not WIDE:
        return np.ones(k)
    levels = np.array([10, -10, 5, -5, 0])
    if group != 512:
        return np.exp2(np.random.permutation(np.resize(levels, k // group))).repeat(group)
    if k % 512:
        return np.exp2(np.random.permutation(np.resize(levels, k // 32))).repeat(32)
    a = np.empty((k // 512, 16))
    for p in range(k // 512):
        a[p, :8] = np.random.permutation(np.resize(levels, 8))
        for g in range(8):
            far = levels[np.abs(levels - a[p, g]) >= 10]
            a[p, g + 8] = far[np.random.randint(len(far))]
    return np.exp2(a.ravel()).repeat(32)


def f64(x):
    return np.asarray(x).astype(np.float64)


H, D, N = 8, 256, 512


def setup_inputs():
    n = np.random.standard_normal
    s = mx_kscale(D, 0)
    u = mx_kscale(N)
    t = np.random.uniform(0.5, 2.0, N) * u
    v = n((H, N, 128))
    v[:, :, 127] = 1.0
    return {
        "q": n((H, D, N)).astype(np.float32),
        "qa": (np.random.uniform(0.5, 2.0, D) * s)[:, None].astype(np.float32),
        "ka": np.tile(np.random.uniform(0.5, 2.0, D) / s, (128, 1)).astype(np.float32),
        "k": n((H, N, D)).astype(np.float32),
        "t": t.reshape(N, 1).astype(np.float32),
        "v": (v / t[:, None]).astype(np.float32),
    }


def reference(q, qa, ka, k, t, v):
    fq = (np.maximum(f64(q), 0.0) + 0.125) * f64(qa)
    fk = (np.maximum(f64(k), 0.0) + 0.125) * f64(t) * f64(ka)[:1]
    S = (mxq(fk, 1, "e4m3").transpose(0, 2, 1) @ mxq(f64(v), 1, "e4m3")) / N
    y = mxq(fq, 1, "e4m3").transpose(0, 2, 1) @ mxq(S, 1, "e4m3")
    y = y / y[:, :, 127:128]
    return y

@@ -1,0 +1,236 @@
+from contextlib import ExitStack
+
+import concourse.mybir as mybir
+
+H, D, N, E = 8, 256, 512, 128
+FLOPS = 2 * H * (D * N * E + N * D * E)
+
+F32 = mybir.dt.float32
+BF16 = mybir.dt.bfloat16
+U32 = mybir.dt.uint32
+U8 = mybir.dt.uint8
+FP8X4 = mybir.dt.float8_e4m3fn_x4
+ACT = mybir.ActivationFunctionType
+ALU = mybir.AluOpType
+
+P = 128
+PACK = 4
+ROWS = 64
+PAIRS = H // 2
+PHI_FLOOR = 0.125
+V_ON_SCALAR = 2
+
+
+def tile_rows_lin_relu1_norm_kernel(tc, q, qa, ka, k, t, v, out):
+    nc = tc.nc
+    with ExitStack() as ctx:
+        keep = ctx.enter_context(tc.tile_pool(name="keep", bufs=1))
+        work = ctx.enter_context(tc.tile_pool(name="work", bufs=PAIRS))
+        psum = ctx.enter_context(tc.psum_pool(name="psum", bufs=1))
+        ctx.enter_context(tc.manual_schedule())
+
+        k_raw = [keep.tile([P, PACK * D], F32, name="k_raw%d" % h) for h in range(H)]
+        q_raw = [keep.tile([P, PACK * N], F32, name="q_raw%d" % g) for g in range(PAIRS)]
+        v_raw = [keep.tile([P, 2, PACK * E], F32, name="v_raw%d" % g) for g in range(PAIRS)]
+        ka_sb = keep.tile([P, D], F32)
+        t_sb = keep.tile([P, PACK], F32)
+        qa_sb = keep.tile([P, PACK], F32)
+        key_weight = keep.tile([P, PACK * D], F32)
+        query_weight = keep.tile([P, ROWS * PACK], F32)
+        k_codes = [keep.tile([P, PACK * 3 * ROWS], U32, name="k_codes%d" % g, align_bytes=64) for g in range(PAIRS)]
+        k_scales = [keep.tile([P, PACK * 3 * ROWS], U8, name="k_scales%d" % g, align_bytes=64) for g in range(PAIRS)]
+
+        q_rows = q.rearrange("h d n -> (h d) n")
+
+        def load_k(h):
+            nc.sync.dma_start(out=k_raw[h][:], in_=k[h].rearrange("(p j) d -> p (j d)", j=PACK))
+
+        def load_v(g):
+            nc.sync.dma_start(out=v_raw[g][:], in_=v[2 * g : 2 * g + 2].rearrange("h (p j) e -> p h (j e)", j=PACK))
+
+        def load_q(g):
+            nc.sync.dma_start(
+                out=q_raw[g][:], in_=q_rows[2 * D * g : 2 * D * (g + 1), :].rearrange("(p j) n -> p (j n)", j=PACK)
+            )
+
+        qa_rows = qa.rearrange("(p j) o -> p (j o)", j=PACK)
+        for c in range(2):
+            nc.scalar.dma_start(out=qa_sb[ROWS * c : ROWS * (c + 1), :], in_=qa_rows)
+        nc.sync.dma_start(out=t_sb[:], in_=t.rearrange("(p j) o -> p (j o)", j=PACK))
+        nc.sync.dma_start(out=ka_sb[:], in_=ka)
+        for g in range(PAIRS):
+            load_k(2 * g)
+            load_k(2 * g + 1)
+            load_v(g)
+            if g > 0:
+                load_q(g - 1)
+        load_q(PAIRS - 1)
+
+        for g in range(PAIRS):
+            nc.vector.memset(k_codes[g][:].rearrange("p (x s m) -> p x s m", x=PACK, s=3)[:, :, 1, :], 0)
+            nc.vector.memset(k_scales[g][:].bitcast(U32).rearrange("p (x s m) -> p x s m", x=PACK, s=3)[:, :, 1, :], 0)
+
+        nc.vector.tensor_tensor(
+            out=key_weight[:].rearrange("p (x m j) -> p x m j", x=PACK, j=PACK),
+            in0=ka_sb[:].rearrange("p (m x) -> p x m", x=PACK).unsqueeze(3).to_broadcast([P, PACK, ROWS, PACK]),
+            in1=t_sb[:].unsqueeze(1).unsqueeze(1).to_broadcast([P, PACK, ROWS, PACK]),
+            op=ALU.mult,
+        )
+
+        def quantize(codes, scales, values):
+            nc.vector.quantize_mx(out=codes.bitcast(FP8X4), scales=scales, in_=values)
+
+        def relu_k(h):
+            relu = work.tile([P, PACK * D], F32, name="k_relu")
+            nc.scalar.activation(
+                out=relu[:].rearrange("p (x m j) -> p m j x", x=PACK, j=PACK),
+                in_=k_raw[h][:].rearrange("p (j m x) -> p m j x", j=PACK, x=PACK),
+                func=ACT.Relu,
+            )
+            return relu
+
+        def weigh_k(relu, k_bf, c):
+            nc.vector.scalar_tensor_tensor(
+                out=k_bf[:].rearrange("p (x c w) -> p x c w", x=PACK, c=2)[:, :, c, :],
+                in0=relu[:].rearrange("p (x w) -> p x w", x=PACK),
+                scalar=PHI_FLOOR,
+                in1=key_weight[:].rearrange("p (x w) -> p x w", x=PACK),
+                op0=ALU.add,
+                op1=ALU.mult,
+            )
+
+        def relu_q(g, u):
+            relu = work.tile([P, PACK * ROWS * PACK], F32, name="q_relu")
+            nc.scalar.activation(
+                out=relu[:].rearrange("p (r m j) -> p m j r", r=PACK, j=PACK),
+                in_=q_raw[g][:].rearrange("p (j m r) -> p m j r", j=PACK, r=PACK)[:, ROWS * u : ROWS * (u + 1)],
+                func=ACT.Relu,
+            )
+            return relu
+
+        def weigh_q(relu, q_bf, u):
+            nc.vector.scalar_tensor_tensor(
+                out=q_bf[:].rearrange("p (r u w) -> p r u w", r=PACK, u=2)[:, :, u, :],
+                in0=relu[:].rearrange("p (r w) -> p r w", r=PACK),
+                scalar=PHI_FLOOR,
+                in1=query_weight[:].unsqueeze(1).to_broadcast([P, PACK, ROWS * PACK]),
+                op0=ALU.add,
+                op1=ALU.mult,
+            )
+
+        nc.vector.tensor_copy(
+            out=query_weight[:].rearrange("p (m j) -> p m j", j=PACK),
+            in_=qa_sb[:].unsqueeze(1).to_broadcast([P, ROWS, PACK]),
+        )
+
+        def pack_v(g):
+            v_bf = work.tile([P, 2 * PACK * E], BF16, align_bytes=64)
+            copy = nc.scalar.copy if g < V_ON_SCALAR else nc.vector.tensor_copy
+            copy(
+                out=v_bf[:].rearrange("p (h c i j) -> p h c j i", h=2, i=PACK, j=PACK),
+                in_=v_raw[g][:].rearrange("p h (j c i) -> p h c j i", j=PACK, i=PACK),
+            )
+            return v_bf
+
+        def build_state(g, k_bf, v_bf):
+            v_codes = work.tile([P, 2 * E], U32, align_bytes=64)
+            v_scales = work.tile([P, 2 * E], U8, align_bytes=64)
+            width = PACK * ROWS
+            for first, run in ((0, 1), (1, 2), (3, 2), (5, 2), (7, 1)):
+                place = first + (first + 1) // 2
+                cols = slice(place * ROWS, (place + run) * ROWS)
+                quantize(k_codes[g][:, cols], k_scales[g][:, cols], k_bf[:, first * width : (first + run) * width])
+            quantize(v_codes[:], v_scales[:], v_bf[:])
+            state = psum.tile([P, PACK, E], F32, name="state", bufs=2)
+            for x in range(PACK):
+                for c in range(2):
+                    cols = slice((3 * x + c) * ROWS, (3 * x + c + 2) * ROWS)
+                    nc.tensor.matmul_mx(
+                        out=state[:, x, :],
+                        lhsT=k_codes[g][:, cols].bitcast(FP8X4),
+                        lhsT_scale=k_scales[g][:, cols],
+                        rhs=v_codes[:, E * c : E * (c + 1)].bitcast(FP8X4),
+                        rhs_scale=v_scales[:, E * c : E * (c + 1)],
+                        start=(c == 0),
+                        stop=(c == 1),
+                    )
+            return state
+
+        def round_state(state):
+            s_bf = work.tile([P, PACK * E], BF16, align_bytes=64)
+            nc.scalar.activation(
+                out=s_bf[:].rearrange("p (e x) -> p e x", x=PACK),
+                in_=state[:].rearrange("p x e -> p e x"),
+                func=ACT.Copy,
+                scale=1.0 / N,
+            )
+            return s_bf
+
+        def read_state(q_bf, s_bf):
+            q_codes = work.tile([P, N], U32, align_bytes=64)
+            q_scales = work.tile([P, N], U8, align_bytes=64)
+            s_codes = work.tile([P, E], U32, align_bytes=64)
+            s_scales = work.tile([P, E], U8, align_bytes=64)
+            quantize(s_codes[:], s_scales[:], s_bf[:])
+            quantize(q_codes[:], q_scales[:], q_bf[:])
+            banks = [psum.tile([P, PACK, E], F32, name="y_bank%d" % c, bufs=3) for c in range(2)]
+            for r in range(PACK):
+                for c in range(2):
+                    rows = slice(ROWS * c, ROWS * (c + 1))
+                    nc.tensor.matmul_mx(
+                        out=banks[c][:, r, :],
+                        lhsT=q_codes[rows, P * r : P * (r + 1)].bitcast(FP8X4),
+                        lhsT_scale=q_scales[rows, P * r : P * (r + 1)],
+                        rhs=s_codes[rows, :].bitcast(FP8X4),
+                        rhs_scale=s_scales[rows, :],
+                        start=True,
+                        stop=True,
+                    )
+            return banks
+
+        def reciprocals(banks):
+            recs = []
+            for c in range(2):
+                rec = work.tile([P, PACK], F32, name="rec%d" % c)
+                nc.vector.reciprocal(out=rec[:], in_=banks[c][:, :, E - 1])
+                recs.append(rec)
+            return recs
+
+        def normalise(h, bank, rec):
+            y = work.tile([P, PACK, E], F32, name="y", bufs=H)
+            if h < H - 1:
+                for r in range(PACK):
+                    nc.scalar.activation(out=y[:, r, :], in_=bank[:, r, :], func=ACT.Copy, scale=rec[:, r : r + 1])
+            else:
+                nc.vector.tensor_tensor(out=y[:], in0=bank[:], in1=rec[:].unsqueeze(2).to_broadcast([P, PACK, E]), op=ALU.mult)
+            nc.sync.dma_start(out=out[h].rearrange("(p r) e -> p r e", r=PACK), in_=y[:])
+
+        banks = {}
+        recs = {}
+        state = None
+        for g in range(-1, PAIRS):
+            nxt = g + 1
+            if nxt < PAIRS:
+                k_bf = work.tile([P, 2 * PACK * D], BF16, align_bytes=64)
+                for c in range(2):
+                    weigh_k(relu_k(2 * nxt + c), k_bf, c)
+                if g >= 1:
+                    recs[g - 1] = reciprocals(banks[g - 1])
+                next_state = build_state(nxt, k_bf, pack_v(nxt))
+            if g >= 0:
+                q_bf = work.tile([P, PACK * N], BF16, align_bytes=64)
+                weigh_q(relu_q(g, 0), q_bf, 0)
+                if nxt == PAIRS:
+                    recs[g - 1] = reciprocals(banks[g - 1])
+                s_bf = round_state(state)
+                weigh_q(relu_q(g, 1), q_bf, 1)
+                banks[g] = read_state(q_bf, s_bf)
+            if g >= 2:
+                for c in range(2):
+                    normalise(2 * (g - 2) + c, banks[g - 2][c], recs[g - 2][c])
+            state = next_state
+        for c in range(2):
+            normalise(H - 4 + c, banks[PAIRS - 2][c], recs[PAIRS - 2][c])
+        recs = reciprocals(banks[PAIRS - 1])
+        for c in range(2):
+            normalise(H - 2 + c, banks[PAIRS - 1][c], recs[c])

@@ -17,8 +17,10 @@ P = 128
 PACK = 4
 ROWS = 64
 PAIRS = H // 2
+LAST = PAIRS - 1
 PHI_FLOOR = 0.125
-V_ON_SCALAR = 2
+KEY_LEAD = 2
+V_ON_SCALAR = ()
 
 
 def tile_rows_lin_relu1_norm_kernel(tc, q, qa, ka, k, t, v, out):
@@ -37,13 +39,15 @@ def tile_rows_lin_relu1_norm_kernel(tc, q, qa, ka, k, t, v, out):
         qa_sb = keep.tile([P, PACK], F32)
         key_weight = keep.tile([P, PACK * D], F32)
         query_weight = keep.tile([P, ROWS * PACK], F32)
-        k_codes = [keep.tile([P, PACK * 3 * ROWS], U32, name="k_codes%d" % g, align_bytes=64) for g in range(PAIRS)]
-        k_scales = [keep.tile([P, PACK * 3 * ROWS], U8, name="k_scales%d" % g, align_bytes=64) for g in range(PAIRS)]
+        windows = 3 * (PACK + 1)
+        k_codes = [keep.tile([P, windows * ROWS], U32, name="k_codes%d" % g, align_bytes=64) for g in range(PAIRS)]
+        k_scales = [keep.tile([P, windows * ROWS], U8, name="k_scales%d" % g, align_bytes=64) for g in range(PAIRS)]
 
         q_rows = q.rearrange("h d n -> (h d) n")
 
-        def load_k(h):
-            nc.sync.dma_start(out=k_raw[h][:], in_=k[h].rearrange("(p j) d -> p (j d)", j=PACK))
+        def load_k(g):
+            for h in (2 * g, 2 * g + 1):
+                nc.sync.dma_start(out=k_raw[h][:], in_=k[h].rearrange("(p j) d -> p (j d)", j=PACK))
 
         def load_v(g):
             nc.sync.dma_start(out=v_raw[g][:], in_=v[2 * g : 2 * g + 2].rearrange("h (p j) e -> p h (j e)", j=PACK))
@@ -56,19 +60,21 @@ def tile_rows_lin_relu1_norm_kernel(tc, q, qa, ka, k, t, v, out):
         qa_rows = qa.rearrange("(p j) o -> p (j o)", j=PACK)
         for c in range(2):
             nc.scalar.dma_start(out=qa_sb[ROWS * c : ROWS * (c + 1), :], in_=qa_rows)
-        nc.sync.dma_start(out=t_sb[:], in_=t.rearrange("(p j) o -> p (j o)", j=PACK))
         nc.sync.dma_start(out=ka_sb[:], in_=ka)
+        nc.sync.dma_start(out=t_sb[:], in_=t.rearrange("(p j) o -> p (j o)", j=PACK))
+        for g in range(KEY_LEAD):
+            load_k(g)
+        load_v(0)
         for g in range(PAIRS):
-            load_k(2 * g)
-            load_k(2 * g + 1)
-            load_v(g)
-            if g > 0:
-                load_q(g - 1)
-        load_q(PAIRS - 1)
+            if g + KEY_LEAD < PAIRS:
+                load_k(g + KEY_LEAD)
+            if g < LAST:
+                load_v(g + 1)
+            load_q(g)
 
         for g in range(PAIRS):
-            nc.vector.memset(k_codes[g][:].rearrange("p (x s m) -> p x s m", x=PACK, s=3)[:, :, 1, :], 0)
-            nc.vector.memset(k_scales[g][:].bitcast(U32).rearrange("p (x s m) -> p x s m", x=PACK, s=3)[:, :, 1, :], 0)
+            nc.vector.memset(k_codes[g][:].rearrange("p (x s m) -> p x s m", s=3, m=ROWS)[:, :, 0, :], 0)
+            nc.vector.memset(k_scales[g][:].bitcast(U32).rearrange("p (x s m) -> p x s m", s=3, m=ROWS // 4)[:, :, 0, :], 0)
 
         nc.vector.tensor_tensor(
             out=key_weight[:].rearrange("p (x m j) -> p x m j", x=PACK, j=PACK),
@@ -77,74 +83,66 @@ def tile_rows_lin_relu1_norm_kernel(tc, q, qa, ka, k, t, v, out):
             op=ALU.mult,
         )
 
-        def quantize(codes, scales, values):
-            nc.vector.quantize_mx(out=codes.bitcast(FP8X4), scales=scales, in_=values)
-
-        def relu_k(h):
-            relu = work.tile([P, PACK * D], F32, name="k_relu")
-            nc.scalar.activation(
-                out=relu[:].rearrange("p (x m j) -> p m j x", x=PACK, j=PACK),
-                in_=k_raw[h][:].rearrange("p (j m x) -> p m j x", j=PACK, x=PACK),
-                func=ACT.Relu,
-            )
-            return relu
-
-        def weigh_k(relu, k_bf, c):
-            nc.vector.scalar_tensor_tensor(
-                out=k_bf[:].rearrange("p (x c w) -> p x c w", x=PACK, c=2)[:, :, c, :],
-                in0=relu[:].rearrange("p (x w) -> p x w", x=PACK),
-                scalar=PHI_FLOOR,
-                in1=key_weight[:].rearrange("p (x w) -> p x w", x=PACK),
-                op0=ALU.add,
-                op1=ALU.mult,
-            )
-
-        def relu_q(g, u):
-            relu = work.tile([P, PACK * ROWS * PACK], F32, name="q_relu")
-            nc.scalar.activation(
-                out=relu[:].rearrange("p (r m j) -> p m j r", r=PACK, j=PACK),
-                in_=q_raw[g][:].rearrange("p (j m r) -> p m j r", j=PACK, r=PACK)[:, ROWS * u : ROWS * (u + 1)],
-                func=ACT.Relu,
-            )
-            return relu
-
-        def weigh_q(relu, q_bf, u):
-            nc.vector.scalar_tensor_tensor(
-                out=q_bf[:].rearrange("p (r u w) -> p r u w", r=PACK, u=2)[:, :, u, :],
-                in0=relu[:].rearrange("p (r w) -> p r w", r=PACK),
-                scalar=PHI_FLOOR,
-                in1=query_weight[:].unsqueeze(1).to_broadcast([P, PACK, ROWS * PACK]),
-                op0=ALU.add,
-                op1=ALU.mult,
-            )
-
         nc.vector.tensor_copy(
             out=query_weight[:].rearrange("p (m j) -> p m j", j=PACK),
             in_=qa_sb[:].unsqueeze(1).to_broadcast([P, ROWS, PACK]),
         )
 
-        def pack_v(g):
+        def quantize(codes, scales, values):
+            nc.vector.quantize_mx(out=codes.bitcast(FP8X4), scales=scales, in_=values)
+
+        def relu_deal(raw, m0, m1, name, bufs):
+            relu = work.tile([P, PACK * (m1 - m0) * PACK], F32, name=name, bufs=bufs)
+            nc.scalar.activation(
+                out=relu[:].rearrange("p (x m j) -> p m j x", x=PACK, j=PACK),
+                in_=raw[:].rearrange("p (j m x) -> p m j x", j=PACK, x=PACK)[:, m0:m1],
+                func=ACT.Relu,
+            )
+            return relu
+
+        def weigh(dst, relu, weight):
+            nc.vector.scalar_tensor_tensor(out=dst, in0=relu, scalar=PHI_FLOOR, in1=weight, op0=ALU.add, op1=ALU.mult)
+
+        k_bf = {}
+
+        def map_keys(g, c):
+            if c == 0:
+                k_bf[g] = work.tile([P, 2 * PACK * D], BF16, name="k_bf", align_bytes=64)
+            parts = 2 if g == 0 else 1
+            step = ROWS // parts
+            for m0 in range(0, ROWS, step):
+                relu = relu_deal(k_raw[2 * g + c], m0, m0 + step, "k_relu", 4)
+                cols = slice(PACK * m0, PACK * (m0 + step))
+                weigh(
+                    k_bf[g][:].rearrange("p (x c w) -> p x c w", x=PACK, c=2)[:, :, 1 - c, cols],
+                    relu[:].rearrange("p (x w) -> p x w", x=PACK),
+                    key_weight[:].rearrange("p (x w) -> p x w", x=PACK)[:, :, cols],
+                )
+
+        def quantize_keys(g):
+            width = 2 * PACK * ROWS
+            for x in range(PACK):
+                cols = slice((3 * x + 1) * ROWS, (3 * x + 3) * ROWS)
+                quantize(k_codes[g][:, cols], k_scales[g][:, cols], k_bf[g][:, x * width : (x + 1) * width])
+
+        def pack_values(g):
             v_bf = work.tile([P, 2 * PACK * E], BF16, align_bytes=64)
-            copy = nc.scalar.copy if g < V_ON_SCALAR else nc.vector.tensor_copy
+            copy = nc.scalar.copy if g in V_ON_SCALAR else nc.vector.tensor_copy
             copy(
                 out=v_bf[:].rearrange("p (h c i j) -> p h c j i", h=2, i=PACK, j=PACK),
                 in_=v_raw[g][:].rearrange("p h (j c i) -> p h c j i", j=PACK, i=PACK),
             )
             return v_bf
 
-        def build_state(g, k_bf, v_bf):
+        def build_state(g, v_bf):
             v_codes = work.tile([P, 2 * E], U32, align_bytes=64)
             v_scales = work.tile([P, 2 * E], U8, align_bytes=64)
-            width = PACK * ROWS
-            for first, run in ((0, 1), (1, 2), (3, 2), (5, 2), (7, 1)):
-                place = first + (first + 1) // 2
-                cols = slice(place * ROWS, (place + run) * ROWS)
-                quantize(k_codes[g][:, cols], k_scales[g][:, cols], k_bf[:, first * width : (first + run) * width])
             quantize(v_codes[:], v_scales[:], v_bf[:])
             state = psum.tile([P, PACK, E], F32, name="state", bufs=2)
             for x in range(PACK):
                 for c in range(2):
-                    cols = slice((3 * x + c) * ROWS, (3 * x + c + 2) * ROWS)
+                    first = 3 * x + 2 * (1 - c)
+                    cols = slice(first * ROWS, (first + 2) * ROWS)
                     nc.tensor.matmul_mx(
                         out=state[:, x, :],
                         lhsT=k_codes[g][:, cols].bitcast(FP8X4),
@@ -166,15 +164,27 @@ def tile_rows_lin_relu1_norm_kernel(tc, q, qa, ka, k, t, v, out):
             )
             return s_bf
 
-        def read_state(q_bf, s_bf):
-            q_codes = work.tile([P, N], U32, align_bytes=64)
-            q_scales = work.tile([P, N], U8, align_bytes=64)
+        def quantize_state(s_bf):
             s_codes = work.tile([P, E], U32, align_bytes=64)
             s_scales = work.tile([P, E], U8, align_bytes=64)
             quantize(s_codes[:], s_scales[:], s_bf[:])
-            quantize(q_codes[:], q_scales[:], q_bf[:])
-            banks = [psum.tile([P, PACK, E], F32, name="y_bank%d" % c, bufs=3) for c in range(2)]
-            for r in range(PACK):
+            return s_codes, s_scales
+
+        def map_queries(g, q_bf, u):
+            relu = relu_deal(q_raw[g], ROWS * u, ROWS * (u + 1), "q_relu", 4)
+            weigh(
+                q_bf[:].rearrange("p (r u w) -> p r u w", r=PACK, u=2)[:, :, u, :],
+                relu[:].rearrange("p (r w) -> p r w", r=PACK),
+                query_weight[:].unsqueeze(1).to_broadcast([P, PACK, ROWS * PACK]),
+            )
+
+        def read_state(q_bf, blocks, s_mx):
+            s_codes, s_scales = s_mx
+            q_codes = work.tile([P, blocks * P], U32, align_bytes=64)
+            q_scales = work.tile([P, blocks * P], U8, align_bytes=64)
+            quantize(q_codes[:], q_scales[:], q_bf)
+            banks = [psum.tile([P, blocks, E], F32, name="y_bank%d" % c, bufs=3) for c in range(2)]
+            for r in range(blocks):
                 for c in range(2):
                     rows = slice(ROWS * c, ROWS * (c + 1))
                     nc.tensor.matmul_mx(
@@ -188,49 +198,94 @@ def tile_rows_lin_relu1_norm_kernel(tc, q, qa, ka, k, t, v, out):
                     )
             return banks
 
-        def reciprocals(banks):
-            recs = []
+        def reciprocal(bank, blocks):
+            rec = work.tile([P, blocks], F32, name="rec", bufs=H + 2)
+            nc.vector.reciprocal(out=rec[:], in_=bank[:, :, E - 1])
+            return rec
+
+        def scale_on_scalar(y, bank, rec, blocks):
+            for r in range(blocks):
+                nc.scalar.activation(out=y[:, r, :], in_=bank[:, r, :], func=ACT.Copy, scale=rec[:, r : r + 1])
+
+        def normalise(g):
             for c in range(2):
-                rec = work.tile([P, PACK], F32, name="rec%d" % c)
-                nc.vector.reciprocal(out=rec[:], in_=banks[c][:, :, E - 1])
-                recs.append(rec)
-            return recs
+                y = work.tile([P, PACK, E], F32, name="y", bufs=H - 2)
+                scale_on_scalar(y, banks[g][c], recs[g][c], PACK)
+                nc.sync.dma_start(out=out[2 * g + c].rearrange("(p r) e -> p r e", r=PACK), in_=y[:])
 
-        def normalise(h, bank, rec):
-            y = work.tile([P, PACK, E], F32, name="y", bufs=H)
-            if h < H - 1:
-                for r in range(PACK):
-                    nc.scalar.activation(out=y[:, r, :], in_=bank[:, r, :], func=ACT.Copy, scale=rec[:, r : r + 1])
+        banks, recs, state, s_mx, q_bf = {}, {}, {}, {}, {}
+
+        for g in range(KEY_LEAD):
+            map_keys(g, 0)
+            map_keys(g, 1)
+            if g == KEY_LEAD - 1:
+                v_bf = pack_values(0)
+            quantize_keys(g)
+        state[0] = build_state(0, v_bf)
+
+        for g in range(LAST):
+            ahead = g + KEY_LEAD
+            q_bf[g] = work.tile([P, PACK * N], BF16, name="q_bf", align_bytes=64)
+            if ahead < PAIRS:
+                map_keys(ahead, 0)
+                if g > 0:
+                    banks[g - 1] = read_state(q_bf[g - 1][:], PACK, s_mx[g - 1])
+                map_keys(ahead, 1)
+                v_bf = pack_values(g + 1)
+                quantize_keys(ahead)
+                state[g + 1] = build_state(g + 1, v_bf)
+                s_bf = round_state(state[g])
+                if g > 0:
+                    recs[g - 1] = [reciprocal(bank, PACK) for bank in banks[g - 1]]
+                map_queries(g, q_bf[g], 0)
+                map_queries(g, q_bf[g], 1)
             else:
-                nc.vector.tensor_tensor(out=y[:], in0=bank[:], in1=rec[:].unsqueeze(2).to_broadcast([P, PACK, E]), op=ALU.mult)
-            nc.sync.dma_start(out=out[h].rearrange("(p r) e -> p r e", r=PACK), in_=y[:])
+                map_queries(g, q_bf[g], 0)
+                v_bf = pack_values(g + 1)
+                banks[g - 1] = read_state(q_bf[g - 1][:], PACK, s_mx[g - 1])
+                state[g + 1] = build_state(g + 1, v_bf)
+                s_bf = round_state(state[g])
+                map_queries(g, q_bf[g], 1)
+                recs[g - 1] = [reciprocal(bank, PACK) for bank in banks[g - 1]]
+            s_mx[g] = quantize_state(s_bf)
+        normalise(0)
 
-        banks = {}
-        recs = {}
-        state = None
-        for g in range(-1, PAIRS):
-            nxt = g + 1
-            if nxt < PAIRS:
-                k_bf = work.tile([P, 2 * PACK * D], BF16, align_bytes=64)
-                for c in range(2):
-                    weigh_k(relu_k(2 * nxt + c), k_bf, c)
-                if g >= 1:
-                    recs[g - 1] = reciprocals(banks[g - 1])
-                next_state = build_state(nxt, k_bf, pack_v(nxt))
-            if g >= 0:
-                q_bf = work.tile([P, PACK * N], BF16, align_bytes=64)
-                weigh_q(relu_q(g, 0), q_bf, 0)
-                if nxt == PAIRS:
-                    recs[g - 1] = reciprocals(banks[g - 1])
-                s_bf = round_state(state)
-                weigh_q(relu_q(g, 1), q_bf, 1)
-                banks[g] = read_state(q_bf, s_bf)
-            if g >= 2:
-                for c in range(2):
-                    normalise(2 * (g - 2) + c, banks[g - 2][c], recs[g - 2][c])
-            state = next_state
-        for c in range(2):
-            normalise(H - 4 + c, banks[PAIRS - 2][c], recs[PAIRS - 2][c])
-        recs = reciprocals(banks[PAIRS - 1])
-        for c in range(2):
-            normalise(H - 2 + c, banks[PAIRS - 1][c], recs[c])
+        relu = relu_deal(q_raw[LAST], 0, P, "q_relu_last", 1)
+        s_bf = round_state(state[LAST])
+        banks[LAST - 1] = read_state(q_bf[LAST - 1][:], PACK, s_mx[LAST - 1])
+        q_last = work.tile([P, PACK * N], BF16, name="q_bf", align_bytes=64)
+        half = PACK * N // 2
+
+        def weigh_last(u):
+            cols = slice(half * u, half * (u + 1))
+            weigh(
+                q_last[:, cols].rearrange("p (a w) -> p a w", a=PACK),
+                relu[:, cols].rearrange("p (a w) -> p a w", a=PACK),
+                query_weight[:].unsqueeze(1).to_broadcast([P, PACK, ROWS * PACK]),
+            )
+
+        out_last = out[H - 2 : H].rearrange("h (p r) e -> p h r e", r=PACK)
+
+        def finish_last(u, y, half_banks, half_recs):
+            nc.vector.tensor_tensor(
+                out=y[:, 1], in0=half_banks[1][:], in1=half_recs[1][:].unsqueeze(2).to_broadcast([P, 2, E]), op=ALU.mult
+            )
+            nc.sync.dma_start(out=out_last[:, :, 2 * u : 2 * u + 2, :], in_=y[:])
+
+        weigh_last(0)
+        s_last = quantize_state(s_bf)
+        recs[LAST - 1] = [reciprocal(bank, PACK) for bank in banks[LAST - 1]]
+        normalise(1)
+        banks_a = read_state(q_last[:, 0:half], 2, s_last)
+        normalise(2)
+        weigh_last(1)
+        recs_a = [reciprocal(bank, 2) for bank in banks_a]
+        y_a = work.tile([P, 2, 2, E], F32, name="y_last", bufs=2)
+        scale_on_scalar(y_a[:, 0], banks_a[0], recs_a[0], 2)
+        banks_b = read_state(q_last[:, half : 2 * half], 2, s_last)
+        finish_last(0, y_a, banks_a, recs_a)
+        rec_b1 = reciprocal(banks_b[1], 2)
+        rec_b0 = reciprocal(banks_b[0], 2)
+        y_b = work.tile([P, 2, 2, E], F32, name="y_last", bufs=2)
+        scale_on_scalar(y_b[:, 0], banks_b[0], rec_b0, 2)
+        finish_last(1, y_b, banks_b, [rec_b0, rec_b1])

@@ -20,7 +20,7 @@ PAIRS = H // 2
 LAST = PAIRS - 1
 PHI_FLOOR = 0.125
 KEY_LEAD = 2
-V_ON_SCALAR = ()
+V_ON_SCALAR = (1,)
 
 
 def tile_rows_lin_relu1_norm_kernel(tc, q, qa, ka, k, t, v, out):
@@ -129,8 +129,8 @@ def tile_rows_lin_relu1_norm_kernel(tc, q, qa, ka, k, t, v, out):
             v_bf = work.tile([P, 2 * PACK * E], BF16, align_bytes=64)
             copy = nc.scalar.copy if g in V_ON_SCALAR else nc.vector.tensor_copy
             copy(
-                out=v_bf[:].rearrange("p (h c i j) -> p h c j i", h=2, i=PACK, j=PACK),
-                in_=v_raw[g][:].rearrange("p h (j c i) -> p h c j i", j=PACK, i=PACK),
+                out=v_bf[:].rearrange("p (h e j) -> p h e j", h=2, j=PACK),
+                in_=v_raw[g][:].rearrange("p h (j e) -> p h e j", j=PACK),
             )
             return v_bf
 
@@ -250,7 +250,15 @@ def tile_rows_lin_relu1_norm_kernel(tc, q, qa, ka, k, t, v, out):
             s_mx[g] = quantize_state(s_bf)
         normalise(0)
 
-        relu = relu_deal(q_raw[LAST], 0, P, "q_relu_last", 1)
+        relus = []
+        for u in range(2):
+            relu = work.tile([P, 2 * P * PACK], F32, name="q_relu", bufs=4)
+            nc.scalar.activation(
+                out=relu[:].rearrange("p (r m j) -> p m j r", r=2, j=PACK),
+                in_=q_raw[LAST][:].rearrange("p (j m r) -> p m j r", j=PACK, r=PACK)[:, :, :, 2 * u : 2 * u + 2],
+                func=ACT.Relu,
+            )
+            relus.append(relu)
         s_bf = round_state(state[LAST])
         banks[LAST - 1] = read_state(q_bf[LAST - 1][:], PACK, s_mx[LAST - 1])
         q_last = work.tile([P, PACK * N], BF16, name="q_bf", align_bytes=64)
@@ -260,7 +268,7 @@ def tile_rows_lin_relu1_norm_kernel(tc, q, qa, ka, k, t, v, out):
             cols = slice(half * u, half * (u + 1))
             weigh(
                 q_last[:, cols].rearrange("p (a w) -> p a w", a=PACK),
-                relu[:, cols].rearrange("p (a w) -> p a w", a=PACK),
+                relus[u][:].rearrange("p (a w) -> p a w", a=PACK),
                 query_weight[:].unsqueeze(1).to_broadcast([P, PACK, ROWS * PACK]),
             )
 

@@ -19,7 +19,7 @@ ROWS = 64
 PAIRS = H // 2
 LAST = PAIRS - 1
 PHI_FLOOR = 0.125
-KEY_LEAD = 2
+STATE_BANKS = 2
 V_ON_SCALAR = (1,)
 
 
@@ -62,14 +62,13 @@ def tile_rows_lin_relu1_norm_kernel(tc, q, qa, ka, k, t, v, out):
             nc.scalar.dma_start(out=qa_sb[ROWS * c : ROWS * (c + 1), :], in_=qa_rows)
         nc.sync.dma_start(out=ka_sb[:], in_=ka)
         nc.sync.dma_start(out=t_sb[:], in_=t.rearrange("(p j) o -> p (j o)", j=PACK))
-        for g in range(KEY_LEAD):
+        for g in range(LAST):
             load_k(g)
-        load_v(0)
-        for g in range(PAIRS):
-            if g + KEY_LEAD < PAIRS:
-                load_k(g + KEY_LEAD)
-            if g < LAST:
-                load_v(g + 1)
+            load_v(g)
+        load_k(LAST)
+        load_q(0)
+        load_v(LAST)
+        for g in range(1, PAIRS):
             load_q(g)
 
         for g in range(PAIRS):
@@ -138,7 +137,7 @@ def tile_rows_lin_relu1_norm_kernel(tc, q, qa, ka, k, t, v, out):
             v_codes = work.tile([P, 2 * E], U32, align_bytes=64)
             v_scales = work.tile([P, 2 * E], U8, align_bytes=64)
             quantize(v_codes[:], v_scales[:], v_bf[:])
-            state = psum.tile([P, PACK, E], F32, name="state", bufs=2)
+            state = psum.tile([P, PACK, E], F32, name="state", bufs=STATE_BANKS)
             for x in range(PACK):
                 for c in range(2):
                     first = 3 * x + 2 * (1 - c)
@@ -199,7 +198,7 @@ def tile_rows_lin_relu1_norm_kernel(tc, q, qa, ka, k, t, v, out):
             return banks
 
         def reciprocal(bank, blocks):
-            rec = work.tile([P, blocks], F32, name="rec", bufs=H + 2)
+            rec = work.tile([P, blocks], F32, name="rec", bufs=H + 4)
             nc.vector.reciprocal(out=rec[:], in_=bank[:, :, E - 1])
             return rec
 
@@ -213,87 +212,76 @@ def tile_rows_lin_relu1_norm_kernel(tc, q, qa, ka, k, t, v, out):
                 scale_on_scalar(y, banks[g][c], recs[g][c], PACK)
                 nc.sync.dma_start(out=out[2 * g + c].rearrange("(p r) e -> p r e", r=PACK), in_=y[:])
 
-        banks, recs, state, s_mx, q_bf = {}, {}, {}, {}, {}
+        banks, recs, state, s_bf = {}, {}, {}, {}
 
-        for g in range(KEY_LEAD):
+        for g in range(PAIRS):
             map_keys(g, 0)
             map_keys(g, 1)
-            if g == KEY_LEAD - 1:
-                v_bf = pack_values(0)
+            if g >= STATE_BANKS:
+                s_bf[g - STATE_BANKS] = round_state(state[g - STATE_BANKS])
+            v_bf = pack_values(g)
             quantize_keys(g)
-        state[0] = build_state(0, v_bf)
+            state[g] = build_state(g, v_bf)
 
         for g in range(LAST):
-            ahead = g + KEY_LEAD
-            q_bf[g] = work.tile([P, PACK * N], BF16, name="q_bf", align_bytes=64)
-            if ahead < PAIRS:
-                map_keys(ahead, 0)
-                if g > 0:
-                    banks[g - 1] = read_state(q_bf[g - 1][:], PACK, s_mx[g - 1])
-                map_keys(ahead, 1)
-                v_bf = pack_values(g + 1)
-                quantize_keys(ahead)
-                state[g + 1] = build_state(g + 1, v_bf)
-                s_bf = round_state(state[g])
-                if g > 0:
-                    recs[g - 1] = [reciprocal(bank, PACK) for bank in banks[g - 1]]
-                map_queries(g, q_bf[g], 0)
-                map_queries(g, q_bf[g], 1)
-            else:
-                map_queries(g, q_bf[g], 0)
-                v_bf = pack_values(g + 1)
-                banks[g - 1] = read_state(q_bf[g - 1][:], PACK, s_mx[g - 1])
-                state[g + 1] = build_state(g + 1, v_bf)
-                s_bf = round_state(state[g])
-                map_queries(g, q_bf[g], 1)
+            q_bf = work.tile([P, PACK * N], BF16, name="q_bf", align_bytes=64)
+            map_queries(g, q_bf, 0)
+            map_queries(g, q_bf, 1)
+            if g + STATE_BANKS < PAIRS:
+                s_bf[g + STATE_BANKS] = round_state(state[g + STATE_BANKS])
+            if g > 0:
                 recs[g - 1] = [reciprocal(bank, PACK) for bank in banks[g - 1]]
-            s_mx[g] = quantize_state(s_bf)
-        normalise(0)
+            banks[g] = read_state(q_bf[:], PACK, quantize_state(s_bf[g]))
 
-        relus = []
-        for u in range(2):
-            relu = work.tile([P, 2 * P * PACK], F32, name="q_relu", bufs=4)
+        q_last = work.tile([P, PACK * N], BF16, name="q_bf", align_bytes=64)
+        out_last = out[H - 2 : H].rearrange("h (p r) e -> p h r e", r=PACK)
+        block = PACK * P
+
+        def relu_last(u):
+            relu = work.tile([P, 2 * block], F32, name="q_relu", bufs=4)
             nc.scalar.activation(
                 out=relu[:].rearrange("p (r m j) -> p m j r", r=2, j=PACK),
                 in_=q_raw[LAST][:].rearrange("p (j m r) -> p m j r", j=PACK, r=PACK)[:, :, :, 2 * u : 2 * u + 2],
                 func=ACT.Relu,
             )
-            relus.append(relu)
-        s_bf = round_state(state[LAST])
-        banks[LAST - 1] = read_state(q_bf[LAST - 1][:], PACK, s_mx[LAST - 1])
-        q_last = work.tile([P, PACK * N], BF16, name="q_bf", align_bytes=64)
-        half = PACK * N // 2
+            return relu
 
-        def weigh_last(u):
-            cols = slice(half * u, half * (u + 1))
+        def weigh_last(relu, r0, r1):
+            width = ROWS * PACK
             weigh(
-                q_last[:, cols].rearrange("p (a w) -> p a w", a=PACK),
-                relus[u][:].rearrange("p (a w) -> p a w", a=PACK),
-                query_weight[:].unsqueeze(1).to_broadcast([P, PACK, ROWS * PACK]),
+                q_last[:, block * r0 : block * r1].rearrange("p (a w) -> p a w", w=width),
+                relu[:, block * (r0 % 2) : block * (r0 % 2 + r1 - r0)].rearrange("p (a w) -> p a w", w=width),
+                query_weight[:].unsqueeze(1).to_broadcast([P, 2 * (r1 - r0), width]),
             )
 
-        out_last = out[H - 2 : H].rearrange("h (p r) e -> p h r e", r=PACK)
+        def read_last(r0, r1):
+            return read_state(q_last[:, block * r0 : block * r1], r1 - r0, s_last)
 
-        def finish_last(u, y, half_banks, half_recs):
+        def reciprocals_last(part, blocks):
+            return [reciprocal(bank, blocks) for bank in part]
+
+        def finish_last(r0, r1, part, part_recs):
+            blocks = r1 - r0
+            y = work.tile([P, 2, blocks, E], F32, name="y_last", bufs=3)
+            scale_on_scalar(y[:, 0], part[0], part_recs[0], blocks)
             nc.vector.tensor_tensor(
-                out=y[:, 1], in0=half_banks[1][:], in1=half_recs[1][:].unsqueeze(2).to_broadcast([P, 2, E]), op=ALU.mult
+                out=y[:, 1], in0=part[1][:], in1=part_recs[1][:].unsqueeze(2).to_broadcast([P, blocks, E]), op=ALU.mult
             )
-            nc.sync.dma_start(out=out_last[:, :, 2 * u : 2 * u + 2, :], in_=y[:])
+            nc.sync.dma_start(out=out_last[:, :, r0:r1, :], in_=y[:])
 
-        weigh_last(0)
-        s_last = quantize_state(s_bf)
-        recs[LAST - 1] = [reciprocal(bank, PACK) for bank in banks[LAST - 1]]
+        normalise(0)
+        weigh_last(relu_last(0), 0, 2)
+        relu = relu_last(1)
         normalise(1)
-        banks_a = read_state(q_last[:, 0:half], 2, s_last)
+        s_last = quantize_state(s_bf[LAST])
+        weigh_last(relu, 2, 3)
+        part_a = read_last(0, 2)
+        recs[LAST - 1] = [reciprocal(bank, PACK) for bank in banks[LAST - 1]]
         normalise(2)
-        weigh_last(1)
-        recs_a = [reciprocal(bank, 2) for bank in banks_a]
-        y_a = work.tile([P, 2, 2, E], F32, name="y_last", bufs=2)
-        scale_on_scalar(y_a[:, 0], banks_a[0], recs_a[0], 2)
-        banks_b = read_state(q_last[:, half : 2 * half], 2, s_last)
-        finish_last(0, y_a, banks_a, recs_a)
-        rec_b1 = reciprocal(banks_b[1], 2)
-        rec_b0 = reciprocal(banks_b[0], 2)
-        y_b = work.tile([P, 2, 2, E], F32, name="y_last", bufs=2)
-        scale_on_scalar(y_b[:, 0], banks_b[0], rec_b0, 2)
-        finish_last(1, y_b, banks_b, [rec_b0, rec_b1])
+        weigh_last(relu, 3, 4)
+        part_b = read_last(2, 3)
+        recs_a = reciprocals_last(part_a, 2)
+        part_c = read_last(3, 4)
+        finish_last(0, 2, part_a, recs_a)
+        finish_last(2, 3, part_b, reciprocals_last(part_b, 1))
+        finish_last(3, 4, part_c, reciprocals_last(part_c, 1))

@@ -20,7 +20,6 @@ PAIRS = H // 2
 LAST = PAIRS - 1
 PHI_FLOOR = 0.125
 STATE_BANKS = 2
-V_ON_SCALAR = (1,)
 
 
 def tile_rows_lin_relu1_norm_kernel(tc, q, qa, ka, k, t, v, out):
@@ -62,14 +61,18 @@ def tile_rows_lin_relu1_norm_kernel(tc, q, qa, ka, k, t, v, out):
             nc.scalar.dma_start(out=qa_sb[ROWS * c : ROWS * (c + 1), :], in_=qa_rows)
         nc.sync.dma_start(out=ka_sb[:], in_=ka)
         nc.sync.dma_start(out=t_sb[:], in_=t.rearrange("(p j) o -> p (j o)", j=PACK))
-        for g in range(LAST):
-            load_k(g)
-            load_v(g)
-        load_k(LAST)
+        load_k(0)
+        load_v(0)
+        load_k(1)
         load_q(0)
-        load_v(LAST)
-        for g in range(1, PAIRS):
-            load_q(g)
+        load_v(1)
+        load_k(2)
+        load_v(2)
+        load_k(3)
+        load_q(1)
+        load_v(3)
+        load_q(2)
+        load_q(3)
 
         for g in range(PAIRS):
             nc.vector.memset(k_codes[g][:].rearrange("p (x s m) -> p x s m", s=3, m=ROWS)[:, :, 0, :], 0)
@@ -126,8 +129,7 @@ def tile_rows_lin_relu1_norm_kernel(tc, q, qa, ka, k, t, v, out):
 
         def pack_values(g):
             v_bf = work.tile([P, 2 * PACK * E], BF16, align_bytes=64)
-            copy = nc.scalar.copy if g in V_ON_SCALAR else nc.vector.tensor_copy
-            copy(
+            nc.vector.tensor_copy(
                 out=v_bf[:].rearrange("p (h e j) -> p h e j", h=2, j=PACK),
                 in_=v_raw[g][:].rearrange("p h (j e) -> p h e j", j=PACK),
             )
@@ -214,23 +216,46 @@ def tile_rows_lin_relu1_norm_kernel(tc, q, qa, ka, k, t, v, out):
 
         banks, recs, state, s_bf = {}, {}, {}, {}
 
-        for g in range(PAIRS):
-            map_keys(g, 0)
-            map_keys(g, 1)
-            if g >= STATE_BANKS:
-                s_bf[g - STATE_BANKS] = round_state(state[g - STATE_BANKS])
+        def state_of(g):
             v_bf = pack_values(g)
             quantize_keys(g)
             state[g] = build_state(g, v_bf)
 
-        for g in range(LAST):
+        def reciprocals(g):
+            recs[g] = [reciprocal(bank, PACK) for bank in banks[g]]
+
+        map_keys(0, 0)
+        map_keys(0, 1)
+        state_of(0)
+
+        map_keys(1, 0)
+        map_keys(1, 1)
+        quantize_keys(1)
+        v_bf = pack_values(1)
+        q_bf = work.tile([P, PACK * N], BF16, name="q_bf", align_bytes=64)
+        map_queries(0, q_bf, 0)
+        state[1] = build_state(1, v_bf)
+        map_queries(0, q_bf, 1)
+        banks[0] = read_state(q_bf[:], PACK, quantize_state(round_state(state[0])))
+
+        map_keys(2, 0)
+        map_keys(2, 1)
+        reciprocals(0)
+        state_of(2)
+
+        map_keys(3, 0)
+        map_keys(3, 1)
+        s_bf[1] = round_state(state[1])
+        normalise(0)
+        state_of(3)
+
+        for g in range(1, LAST):
             q_bf = work.tile([P, PACK * N], BF16, name="q_bf", align_bytes=64)
             map_queries(g, q_bf, 0)
             map_queries(g, q_bf, 1)
-            if g + STATE_BANKS < PAIRS:
-                s_bf[g + STATE_BANKS] = round_state(state[g + STATE_BANKS])
-            if g > 0:
-                recs[g - 1] = [reciprocal(bank, PACK) for bank in banks[g - 1]]
+            s_bf[g + 1] = round_state(state[g + 1])
+            if g > 1:
+                reciprocals(g - 1)
             banks[g] = read_state(q_bf[:], PACK, quantize_state(s_bf[g]))
 
         q_last = work.tile([P, PACK * N], BF16, name="q_bf", align_bytes=64)
@@ -269,15 +294,14 @@ def tile_rows_lin_relu1_norm_kernel(tc, q, qa, ka, k, t, v, out):
             )
             nc.sync.dma_start(out=out_last[:, :, r0:r1, :], in_=y[:])
 
-        normalise(0)
         weigh_last(relu_last(0), 0, 2)
         relu = relu_last(1)
         normalise(1)
         s_last = quantize_state(s_bf[LAST])
-        weigh_last(relu, 2, 3)
         part_a = read_last(0, 2)
-        recs[LAST - 1] = [reciprocal(bank, PACK) for bank in banks[LAST - 1]]
+        reciprocals(LAST - 1)
         normalise(2)
+        weigh_last(relu, 2, 3)
         weigh_last(relu, 3, 4)
         part_b = read_last(2, 3)
         recs_a = reciprocals_last(part_a, 2)

from contextlib import ExitStack

import concourse.mybir as mybir

H, D, N, E = 8, 256, 512, 128
FLOPS = 2 * H * (D * N * E + N * D * E)

F32 = mybir.dt.float32
BF16 = mybir.dt.bfloat16
U32 = mybir.dt.uint32
U8 = mybir.dt.uint8
FP8X4 = mybir.dt.float8_e4m3fn_x4
ACT = mybir.ActivationFunctionType
ALU = mybir.AluOpType

P = 128
PACK = 4
ROWS = 64
PAIRS = H // 2
LAST = PAIRS - 1
PHI_FLOOR = 0.125
STATE_BANKS = 2


def tile_rows_lin_relu1_norm_kernel(tc, q, qa, ka, k, t, v, out):
    nc = tc.nc
    with ExitStack() as ctx:
        keep = ctx.enter_context(tc.tile_pool(name="keep", bufs=1))
        work = ctx.enter_context(tc.tile_pool(name="work", bufs=PAIRS))
        psum = ctx.enter_context(tc.psum_pool(name="psum", bufs=1))
        ctx.enter_context(tc.manual_schedule())

        k_raw = [keep.tile([P, PACK * D], F32, name="k_raw%d" % h) for h in range(H)]
        q_raw = [keep.tile([P, PACK * N], F32, name="q_raw%d" % g) for g in range(PAIRS)]
        v_raw = [keep.tile([P, 2, PACK * E], F32, name="v_raw%d" % g) for g in range(PAIRS)]
        ka_sb = keep.tile([P, D], F32)
        t_sb = keep.tile([P, PACK], F32)
        qa_sb = keep.tile([P, PACK], F32)
        key_weight = keep.tile([P, PACK * D], F32)
        query_weight = keep.tile([P, ROWS * PACK], F32)
        windows = 3 * (PACK + 1)
        k_codes = [keep.tile([P, windows * ROWS], U32, name="k_codes%d" % g, align_bytes=64) for g in range(PAIRS)]
        k_scales = [keep.tile([P, windows * ROWS], U8, name="k_scales%d" % g, align_bytes=64) for g in range(PAIRS)]

        q_rows = q.rearrange("h d n -> (h d) n")

        def load_k(g):
            for h in (2 * g, 2 * g + 1):
                nc.sync.dma_start(out=k_raw[h][:], in_=k[h].rearrange("(p j) d -> p (j d)", j=PACK))

        def load_v(g):
            nc.sync.dma_start(out=v_raw[g][:], in_=v[2 * g : 2 * g + 2].rearrange("h (p j) e -> p h (j e)", j=PACK))

        def load_q(g):
            nc.sync.dma_start(
                out=q_raw[g][:], in_=q_rows[2 * D * g : 2 * D * (g + 1), :].rearrange("(p j) n -> p (j n)", j=PACK)
            )

        qa_rows = qa.rearrange("(p j) o -> p (j o)", j=PACK)
        for c in range(2):
            nc.scalar.dma_start(out=qa_sb[ROWS * c : ROWS * (c + 1), :], in_=qa_rows)
        nc.sync.dma_start(out=ka_sb[:], in_=ka)
        nc.sync.dma_start(out=t_sb[:], in_=t.rearrange("(p j) o -> p (j o)", j=PACK))
        load_k(0)
        load_v(0)
        load_k(1)
        load_q(0)
        load_v(1)
        load_k(2)
        load_v(2)
        load_k(3)
        load_q(1)
        load_v(3)
        load_q(2)
        load_q(3)

        for g in range(PAIRS):
            nc.vector.memset(k_codes[g][:].rearrange("p (x s m) -> p x s m", s=3, m=ROWS)[:, :, 0, :], 0)
            nc.vector.memset(k_scales[g][:].bitcast(U32).rearrange("p (x s m) -> p x s m", s=3, m=ROWS // 4)[:, :, 0, :], 0)

        nc.vector.tensor_tensor(
            out=key_weight[:].rearrange("p (x m j) -> p x m j", x=PACK, j=PACK),
            in0=ka_sb[:].rearrange("p (m x) -> p x m", x=PACK).unsqueeze(3).to_broadcast([P, PACK, ROWS, PACK]),
            in1=t_sb[:].unsqueeze(1).unsqueeze(1).to_broadcast([P, PACK, ROWS, PACK]),
            op=ALU.mult,
        )

        nc.vector.tensor_copy(
            out=query_weight[:].rearrange("p (m j) -> p m j", j=PACK),
            in_=qa_sb[:].unsqueeze(1).to_broadcast([P, ROWS, PACK]),
        )

        def quantize(codes, scales, values):
            nc.vector.quantize_mx(out=codes.bitcast(FP8X4), scales=scales, in_=values)

        def relu_deal(raw, m0, m1, name, bufs):
            relu = work.tile([P, PACK * (m1 - m0) * PACK], F32, name=name, bufs=bufs)
            nc.scalar.activation(
                out=relu[:].rearrange("p (x m j) -> p m j x", x=PACK, j=PACK),
                in_=raw[:].rearrange("p (j m x) -> p m j x", j=PACK, x=PACK)[:, m0:m1],
                func=ACT.Relu,
            )
            return relu

        def weigh(dst, relu, weight):
            nc.vector.scalar_tensor_tensor(out=dst, in0=relu, scalar=PHI_FLOOR, in1=weight, op0=ALU.add, op1=ALU.mult)

        k_bf = {}

        def map_keys(g, c):
            if c == 0:
                k_bf[g] = work.tile([P, 2 * PACK * D], BF16, name="k_bf", align_bytes=64)
            parts = 2 if g == 0 else 1
            step = ROWS // parts
            for m0 in range(0, ROWS, step):
                relu = relu_deal(k_raw[2 * g + c], m0, m0 + step, "k_relu", 4)
                cols = slice(PACK * m0, PACK * (m0 + step))
                weigh(
                    k_bf[g][:].rearrange("p (x c w) -> p x c w", x=PACK, c=2)[:, :, 1 - c, cols],
                    relu[:].rearrange("p (x w) -> p x w", x=PACK),
                    key_weight[:].rearrange("p (x w) -> p x w", x=PACK)[:, :, cols],
                )

        def quantize_keys(g):
            width = 2 * PACK * ROWS
            for x in range(PACK):
                cols = slice((3 * x + 1) * ROWS, (3 * x + 3) * ROWS)
                quantize(k_codes[g][:, cols], k_scales[g][:, cols], k_bf[g][:, x * width : (x + 1) * width])

        def pack_values(g):
            v_bf = work.tile([P, 2 * PACK * E], BF16, align_bytes=64)
            nc.vector.tensor_copy(
                out=v_bf[:].rearrange("p (h e j) -> p h e j", h=2, j=PACK),
                in_=v_raw[g][:].rearrange("p h (j e) -> p h e j", j=PACK),
            )
            return v_bf

        def build_state(g, v_bf):
            v_codes = work.tile([P, 2 * E], U32, align_bytes=64)
            v_scales = work.tile([P, 2 * E], U8, align_bytes=64)
            quantize(v_codes[:], v_scales[:], v_bf[:])
            state = psum.tile([P, PACK, E], F32, name="state", bufs=STATE_BANKS)
            for x in range(PACK):
                for c in range(2):
                    first = 3 * x + 2 * (1 - c)
                    cols = slice(first * ROWS, (first + 2) * ROWS)
                    nc.tensor.matmul_mx(
                        out=state[:, x, :],
                        lhsT=k_codes[g][:, cols].bitcast(FP8X4),
                        lhsT_scale=k_scales[g][:, cols],
                        rhs=v_codes[:, E * c : E * (c + 1)].bitcast(FP8X4),
                        rhs_scale=v_scales[:, E * c : E * (c + 1)],
                        start=(c == 0),
                        stop=(c == 1),
                    )
            return state

        def round_state(state):
            s_bf = work.tile([P, PACK * E], BF16, align_bytes=64)
            nc.scalar.activation(
                out=s_bf[:].rearrange("p (e x) -> p e x", x=PACK),
                in_=state[:].rearrange("p x e -> p e x"),
                func=ACT.Copy,
                scale=1.0 / N,
            )
            return s_bf

        def quantize_state(s_bf):
            s_codes = work.tile([P, E], U32, align_bytes=64)
            s_scales = work.tile([P, E], U8, align_bytes=64)
            quantize(s_codes[:], s_scales[:], s_bf[:])
            return s_codes, s_scales

        def map_queries(g, q_bf, u):
            relu = relu_deal(q_raw[g], ROWS * u, ROWS * (u + 1), "q_relu", 4)
            weigh(
                q_bf[:].rearrange("p (r u w) -> p r u w", r=PACK, u=2)[:, :, u, :],
                relu[:].rearrange("p (r w) -> p r w", r=PACK),
                query_weight[:].unsqueeze(1).to_broadcast([P, PACK, ROWS * PACK]),
            )

        def read_state(q_bf, blocks, s_mx):
            s_codes, s_scales = s_mx
            q_codes = work.tile([P, blocks * P], U32, align_bytes=64)
            q_scales = work.tile([P, blocks * P], U8, align_bytes=64)
            quantize(q_codes[:], q_scales[:], q_bf)
            banks = [psum.tile([P, blocks, E], F32, name="y_bank%d" % c, bufs=3) for c in range(2)]
            for r in range(blocks):
                for c in range(2):
                    rows = slice(ROWS * c, ROWS * (c + 1))
                    nc.tensor.matmul_mx(
                        out=banks[c][:, r, :],
                        lhsT=q_codes[rows, P * r : P * (r + 1)].bitcast(FP8X4),
                        lhsT_scale=q_scales[rows, P * r : P * (r + 1)],
                        rhs=s_codes[rows, :].bitcast(FP8X4),
                        rhs_scale=s_scales[rows, :],
                        start=True,
                        stop=True,
                    )
            return banks

        def reciprocal(bank, blocks):
            rec = work.tile([P, blocks], F32, name="rec", bufs=H + 4)
            nc.vector.reciprocal(out=rec[:], in_=bank[:, :, E - 1])
            return rec

        def scale_on_scalar(y, bank, rec, blocks):
            for r in range(blocks):
                nc.scalar.activation(out=y[:, r, :], in_=bank[:, r, :], func=ACT.Copy, scale=rec[:, r : r + 1])

        def normalise(g):
            for c in range(2):
                y = work.tile([P, PACK, E], F32, name="y", bufs=H - 2)
                scale_on_scalar(y, banks[g][c], recs[g][c], PACK)
                nc.sync.dma_start(out=out[2 * g + c].rearrange("(p r) e -> p r e", r=PACK), in_=y[:])

        banks, recs, state, s_bf = {}, {}, {}, {}

        def state_of(g):
            v_bf = pack_values(g)
            quantize_keys(g)
            state[g] = build_state(g, v_bf)

        def reciprocals(g):
            recs[g] = [reciprocal(bank, PACK) for bank in banks[g]]

        map_keys(0, 0)
        map_keys(0, 1)
        state_of(0)

        map_keys(1, 0)
        map_keys(1, 1)
        quantize_keys(1)
        v_bf = pack_values(1)
        q_bf = work.tile([P, PACK * N], BF16, name="q_bf", align_bytes=64)
        map_queries(0, q_bf, 0)
        state[1] = build_state(1, v_bf)
        map_queries(0, q_bf, 1)
        banks[0] = read_state(q_bf[:], PACK, quantize_state(round_state(state[0])))

        map_keys(2, 0)
        map_keys(2, 1)
        reciprocals(0)
        state_of(2)

        map_keys(3, 0)
        map_keys(3, 1)
        s_bf[1] = round_state(state[1])
        normalise(0)
        state_of(3)

        for g in range(1, LAST):
            q_bf = work.tile([P, PACK * N], BF16, name="q_bf", align_bytes=64)
            map_queries(g, q_bf, 0)
            map_queries(g, q_bf, 1)
            s_bf[g + 1] = round_state(state[g + 1])
            if g > 1:
                reciprocals(g - 1)
            banks[g] = read_state(q_bf[:], PACK, quantize_state(s_bf[g]))

        q_last = work.tile([P, PACK * N], BF16, name="q_bf", align_bytes=64)
        out_last = out[H - 2 : H].rearrange("h (p r) e -> p h r e", r=PACK)
        block = PACK * P

        def relu_last(u):
            relu = work.tile([P, 2 * block], F32, name="q_relu", bufs=4)
            nc.scalar.activation(
                out=relu[:].rearrange("p (r m j) -> p m j r", r=2, j=PACK),
                in_=q_raw[LAST][:].rearrange("p (j m r) -> p m j r", j=PACK, r=PACK)[:, :, :, 2 * u : 2 * u + 2],
                func=ACT.Relu,
            )
            return relu

        def weigh_last(relu, r0, r1):
            width = ROWS * PACK
            weigh(
                q_last[:, block * r0 : block * r1].rearrange("p (a w) -> p a w", w=width),
                relu[:, block * (r0 % 2) : block * (r0 % 2 + r1 - r0)].rearrange("p (a w) -> p a w", w=width),
                query_weight[:].unsqueeze(1).to_broadcast([P, 2 * (r1 - r0), width]),
            )

        def read_last(r0, r1):
            return read_state(q_last[:, block * r0 : block * r1], r1 - r0, s_last)

        def reciprocals_last(part, blocks):
            return [reciprocal(bank, blocks) for bank in part]

        def finish_last(r0, r1, part, part_recs):
            blocks = r1 - r0
            y = work.tile([P, 2, blocks, E], F32, name="y_last", bufs=3)
            scale_on_scalar(y[:, 0], part[0], part_recs[0], blocks)
            nc.vector.tensor_tensor(
                out=y[:, 1], in0=part[1][:], in1=part_recs[1][:].unsqueeze(2).to_broadcast([P, blocks, E]), op=ALU.mult
            )
            nc.sync.dma_start(out=out_last[:, :, r0:r1, :], in_=y[:])

        weigh_last(relu_last(0), 0, 2)
        relu = relu_last(1)
        normalise(1)
        s_last = quantize_state(s_bf[LAST])
        part_a = read_last(0, 2)
        reciprocals(LAST - 1)
        normalise(2)
        weigh_last(relu, 2, 3)
        weigh_last(relu, 3, 4)
        part_b = read_last(2, 3)
        recs_a = reciprocals_last(part_a, 2)
        part_c = read_last(3, 4)
        finish_last(0, 2, part_a, recs_a)
        finish_last(2, 3, part_b, reciprocals_last(part_b, 1))
        finish_last(3, 4, part_c, reciprocals_last(part_c, 1))
